import numpy as np
import ml_dtypes


def mxq(x, axis, fmt="e4m3"):
    dtype, down = {"e4m3": (ml_dtypes.float8_e4m3fn, 7), "e5m2": (ml_dtypes.float8_e5m2, 14)}[fmt]
    v = np.moveaxis(np.asarray(x, np.float32).astype(ml_dtypes.bfloat16).astype(np.float64), axis, -1)
    blocks = v.reshape(v.shape[:-1] + (-1, 32))
    amax = np.abs(blocks).max(-1, keepdims=True)
    byte = np.maximum(np.where(amax > 0, np.frexp(amax)[1] - 1 + 127, 0) - down, 1)
    scale = np.exp2(byte - 127.0)
    codes = (blocks / scale).astype(np.float32).astype(dtype).astype(np.float64)
    return np.moveaxis((codes * scale).reshape(v.shape), -1, axis)


WIDE = False


def mx_kscale(k):
    if not WIDE:
        return np.ones(k)
    levels = np.array([10, -10, 5, -5, 0])
    if k % 512:
        return np.exp2(np.random.permutation(np.resize(levels, k // 32))).repeat(32)
    a = np.empty((k // 512, 16))
    for p in range(k // 512):
        a[p, :8] = np.random.permutation(np.resize(levels, 8))
        for g in range(8):
            far = levels[np.abs(levels - a[p, g]) >= 10]
            a[p, g + 8] = far[np.random.randint(len(far))]
    return np.exp2(a.ravel()).repeat(32)


def f64(x):
    return np.asarray(x).astype(np.float64)


def striped(idx):
    return np.tile(idx.reshape(-1, 16).T, (8, 1)).astype(np.uint16)


def unstriped(offs):
    return offs[:16].T.reshape(-1).astype(np.int64)


def striped8(idx):
    return np.concatenate([x.reshape(-1, 16).T for x in idx]).astype(np.uint16)


def runs(offs, k):
    lists = np.stack([offs[16 * r : 16 * r + 16].T.reshape(-1) for r in range(8)]).astype(np.int64)
    return lists[np.arange(k) % 512 // 64]


def pack_weight(w):
    k, n = w.shape
    w = f64(np.asarray(w, np.float32).astype(ml_dtypes.bfloat16)).reshape(k // 32, 32, n)
    amax = np.abs(w).max(1)
    byte = np.clip(np.where(amax > 0, np.frexp(amax)[1] - 1 + 127 - 7, 1), 1, 254)
    scaled = (w * np.exp2(127.0 - byte)[:, None, :]).reshape(k, n).astype(np.float32)
    words = np.ascontiguousarray(scaled.reshape(k // 512, 128, 4, n).transpose(0, 1, 3, 2)).astype(ml_dtypes.float8_e4m3fn).view(np.uint8)
    return words, np.ascontiguousarray(byte.astype(np.uint8).reshape(k // 512, 16, n))


def unpack_weight(words, scales):
    g, p, n, _ = words.shape
    vals = np.ascontiguousarray(words).view(ml_dtypes.float8_e4m3fn).astype(np.float64) * np.repeat(np.exp2(scales.astype(np.float64) - 127.0), 8, axis=1)[..., None]
    return vals.transpose(0, 1, 3, 2).reshape(g * 512, n)


def relu(v):
    return np.maximum(v, 0.0)


K, T, S, N, H = 512, 2048, 512, 512, 512


def setup_inputs():
    n = np.random.standard_normal
    s = mx_kscale(K)[:, None]
    u = mx_kscale(H)
    packed_xT = pack_weight(n((K, T)) * s)
    return {
        "x_words": packed_xT[0],
        "x_scales": packed_xT[1],
        "w1": (n((K, H)) / np.sqrt(K) / s).astype(np.float32),
        "w2": (n((K, H)) / np.sqrt(K) / s).astype(np.float32),
        "gn": (np.random.uniform(0.5, 1.5, (H, 1)) * u[:, None]).astype(np.float32),
        "w3": (n((H, N)) / np.sqrt(H) / u[:, None]).astype(np.float32),
        "res": (2 * n((N, S))).astype(np.float32),
        "offs": striped(np.random.permutation(T)[:S]),
        "two": striped(np.random.permutation(T)[:S]),
        "lf": striped8(np.stack([np.random.permutation(S) for _ in range(8)])),
        "rt": striped8(np.stack([np.random.permutation(S) for _ in range(8)])),
    }


def reference(x_words, x_scales, w1, w2, gn, w3, res, offs, two, lf, rt):
    x_two = unpack_weight(x_words, x_scales)[:, unstriped(two)]
    c = mxq(f64(w2), 0, "e4m3").T @ x_two
    xq = unpack_weight(x_words, x_scales)[:, unstriped(offs)]
    y = mxq(f64(w1), 0, "e4m3").T @ xq
    z = f64(gn) * (-0.75 * (relu(c) * (y - (y[np.arange(H)[:, None], runs(lf, H)])) + (c - relu(c)) * (y[np.arange(H)[:, None], runs(rt, H)] - y)))
    return f64(res) + (mxq(f64(w3), 0, "e4m3").T @ mxq(z, 0, "e4m3"))

@@ -1,0 +1,214 @@
+from contextlib import ExitStack
+
+import concourse.mybir as mybir
+
+K, T, S, H, N = 512, 2048, 512, 512, 512
+FLOPS = 2 * K * H * S * 2 + 2 * H * N * S
+
+F32 = mybir.dt.float32
+BF16 = mybir.dt.bfloat16
+I32 = mybir.dt.int32
+U32 = mybir.dt.uint32
+U16 = mybir.dt.uint16
+U8 = mybir.dt.uint8
+FP8X4 = mybir.dt.float8_e4m3fn_x4
+ALU = mybir.AluOpType
+COPY = mybir.ActivationFunctionType.Copy
+
+P = 128
+PACK = 4
+HALF = 256
+BLK = 128
+NBLK = S // BLK
+LIST = 16
+
+
+def tile_picked_upwind2_none_p_kernel(
+    tc, x_words, x_scales, w1, w2, gn, w3, res, offs, two, lf, rt, out
+):
+    nc = tc.nc
+    with ExitStack() as ctx:
+        keep = ctx.enter_context(tc.tile_pool(name="keep", bufs=1))
+        psum = ctx.enter_context(tc.psum_pool(name="psum", bufs=1))
+
+        def tile(name, shape, dtype):
+            return keep.tile(shape, dtype, name=name, align_bytes=64)
+
+        def bank(i, shape):
+            return psum.tile(shape, F32, name="bank%d" % i, tag="bank%d" % i)
+
+        offs_t = tile("offs_t", [P, S // LIST], U16)
+        two_t = tile("two_t", [P, S // LIST], U16)
+        lf_t = tile("lf_t", [P, S // LIST], U16)
+        rt_t = tile("rt_t", [P, S // LIST], U16)
+        xw = tile("xw", [P, T], U32)
+        xs = tile("xs", [P, T], U8)
+        gain = tile("gain", [P, PACK], F32)
+
+        nc.vector.memset(xs[:].bitcast(I32), 0)
+        nc.sync.dma_start(offs_t[:], offs)
+        for q in range(4):
+            nc.sync.dma_start(xs[32 * q : 32 * q + 4, :].bitcast(I32), x_scales[0, 4 * q : 4 * q + 4, :].bitcast(I32))
+        nc.sync.dma_start(two_t[:], two)
+        nc.gpsimd.dma_start(gain[:], gn.rearrange("(p t) o -> p (t o)", t=PACK))
+
+        def load_halves(name, w):
+            halves = []
+            rows = w.rearrange("(p j) c -> p j c", j=PACK)
+            for h in range(2):
+                raw = tile("%s_raw%d" % (name, h), [P, PACK, HALF], F32)
+                nc.sync.dma_start(raw[:], rows[:, :, h * HALF : (h + 1) * HALF])
+                halves.append(raw)
+            return halves
+
+        w1_raw = load_halves("w1", w1)
+        nc.sync.dma_start(xw[:].bitcast(I32), x_words[0].rearrange("p n t -> p (n t)").bitcast(I32))
+        nc.sync.dma_start(lf_t[:], lf)
+        nc.sync.dma_start(rt_t[:], rt)
+        w2_raw = load_halves("w2", w2)
+        w3_raw = load_halves("w3", w3)
+        res_t = tile("res_t", [P, PACK, S], F32)
+        nc.sync.dma_start(res_t[:], res.rearrange("(g p) j -> p g j", p=P))
+
+        def deal(name, raw, u):
+            dealt = tile("%s_bf%d" % (name, u), [P, 2, P, PACK], BF16)
+            for h in range(2):
+                nc.scalar.copy(
+                    dealt[:].rearrange("p e m j -> p m j e")[:, 64 * h : 64 * h + 64],
+                    raw[h][:].rearrange("p j (m u e) -> p u m j e", u=2, e=2)[:, u],
+                )
+            return dealt
+
+        def quantize(name, src, width):
+            codes = tile(name + "_codes", [P, width], U32)
+            scales = tile(name + "_scales", [P, width], U8)
+            nc.vector.quantize_mx(out=codes[:].bitcast(FP8X4), scales=scales[:], in_=src)
+            return codes, scales
+
+        def product(dst, lhs, lhs_cols, rhs, rhs_cols):
+            nc.tensor.matmul_mx(
+                out=dst,
+                lhsT=lhs[0][:, lhs_cols].bitcast(FP8X4),
+                lhsT_scale=lhs[1][:, lhs_cols],
+                rhs=rhs[0][:, rhs_cols].bitcast(FP8X4),
+                rhs_scale=rhs[1][:, rhs_cols],
+                start=True,
+                stop=True,
+            )
+
+        xq = (tile("xq_w", [P, S], U32), tile("xq_s", [P, S], U8))
+        x2 = (tile("x2_w", [P, S], U32), tile("x2_s", [P, S], U8))
+        nc.vector.tensor_copy(xq[1][:], xs[:].indirect(offs_t[:]))
+        nc.vector.tensor_copy(x2[1][:], xs[:].indirect(two_t[:]))
+
+        gpos = tile("gpos", [P, PACK], F32)
+        gneg = tile("gneg", [P, PACK], F32)
+        nc.vector.tensor_scalar(gpos[:], gain[:], 0.75, None, ALU.mult)
+        nc.vector.tensor_scalar(gneg[:], gain[:], -0.75, None, ALU.mult)
+
+        w1_bf = [deal("w1", w1_raw, u) for u in range(2)]
+        w1q = [quantize("w1q%d" % u, w1_bf[u][:].rearrange("p e m j -> p (e m j)"), HALF) for u in range(2)]
+        nc.vector.tensor_copy(xq[0][:], xw[:].indirect(offs_t[:]))
+        nc.vector.tensor_copy(x2[0][:], xw[:].indirect(two_t[:]))
+
+        ypos, yneg = [], []
+        for t in range(PACK):
+            y = bank(t, [P, S])
+            product(y[:], w1q[t // 2], slice(P * (t % 2), P * (t % 2 + 1)), xq, slice(0, S))
+            yp = tile("ypos%d" % t, [P, S], F32)
+            yn = tile("yneg%d" % t, [P, S], F32)
+            nc.scalar.activation(yp[:], y[:], COPY, scale=gpos[:, t : t + 1])
+            nc.scalar.activation(yn[:], y[:], COPY, scale=gneg[:, t : t + 1])
+            ypos.append(yp)
+            yneg.append(yn)
+
+        dl = tile("dl", [P, PACK, S], F32)
+        dr = tile("dr", [P, PACK, S], F32)
+
+        def left(t, a, b):
+            nc.vector.tensor_tensor(dl[:, t, a:b], ypos[t][:].indirect(lf_t[:, a // LIST : b // LIST]), yneg[t][:, a:b], ALU.add)
+
+        def right(t, a, b):
+            nc.vector.tensor_tensor(dr[:, t, a:b], yneg[t][:].indirect(rt_t[:, a // LIST : b // LIST]), ypos[t][:, a:b], ALU.add)
+
+        def differences(t):
+            for h in range(2):
+                left(t, h * HALF, (h + 1) * HALF)
+                right(t, h * HALF, (h + 1) * HALF)
+
+        w2_bf = [deal("w2", w2_raw, u) for u in range(2)]
+        w3_bf = tile("w3_bf", [P, N, PACK], BF16)
+        for h in range(2):
+            nc.scalar.copy(
+                w3_bf[:, h * HALF : (h + 1) * HALF, :].rearrange("p (c i) j -> p c j i", i=4),
+                w3_raw[h][:].rearrange("p j (c i) -> p c j i", i=4),
+            )
+
+        differences(0)
+        differences(1)
+        w2q = [quantize("w2q%d" % u, w2_bf[u][:].rearrange("p e m j -> p (e m j)"), HALF) for u in range(2)]
+        wind = []
+        for b in range(NBLK):
+            c = bank(PACK + b, [P, PACK, BLK])
+            for t in range(PACK):
+                product(c[:, t, :], w2q[t // 2], slice(P * (t % 2), P * (t % 2 + 1)), x2, slice(b * BLK, (b + 1) * BLK))
+            wind.append(c)
+        differences(2)
+        w3q = quantize("w3q", w3_bf[:].rearrange("p n j -> p (n j)"), N)
+
+        from_left, from_right, z_bf, sums = {}, {}, {}, {}
+
+        def cols(b):
+            return slice(b * BLK, (b + 1) * BLK)
+
+        def term_left(b):
+            from_left[b] = tile("from_left%d" % b, [P, PACK, BLK], F32)
+            nc.vector.scalar_tensor_tensor(from_left[b][:], wind[b][:], 0.0, dl[:, :, cols(b)], ALU.max, ALU.mult)
+
+        def term_right(b):
+            from_right[b] = tile("from_right%d" % b, [P, PACK, BLK], F32)
+            nc.vector.scalar_tensor_tensor(from_right[b][:], wind[b][:], 0.0, dr[:, :, cols(b)], ALU.min, ALU.mult)
+
+        def change(b):
+            z_bf[b] = tile("z_bf%d" % b, [P, BLK, PACK], BF16)
+            nc.vector.tensor_tensor(
+                z_bf[b][:].rearrange("p (c i) t -> p c t i", i=2),
+                from_left[b][:].rearrange("p t (c i) -> p c t i", i=2),
+                from_right[b][:].rearrange("p t (c i) -> p c t i", i=2),
+                ALU.add,
+            )
+
+        def last_product(b):
+            zq = quantize("zq%d" % b, z_bf[b][:].rearrange("p j t -> p (j t)"), BLK)
+            sums[b] = bank(b, [P, PACK, BLK])
+            for g in range(PACK):
+                product(sums[b][:, g, :], w3q, slice(P * g, P * (g + 1)), zq, slice(0, BLK))
+
+        def finish(b):
+            o = tile("o%d" % b, [P, PACK, BLK], F32)
+            nc.vector.tensor_tensor(o[:], sums[b][:], res_t[:, :, cols(b)], ALU.add)
+            nc.sync.dma_start(out.rearrange("(g p) j -> p g j", p=P)[:, :, cols(b)], o[:])
+
+        last = PACK - 1
+        for b in range(2):
+            left(last, b * BLK, (b + 1) * BLK)
+            right(last, b * BLK, (b + 1) * BLK)
+        for b in range(2):
+            term_left(b)
+            term_right(b)
+            left(last, (b + 2) * BLK, (b + 3) * BLK)
+            change(b)
+            right(last, (b + 2) * BLK, (b + 3) * BLK)
+            last_product(b)
+        term_left(2)
+        term_right(2)
+        term_left(3)
+        change(2)
+        term_right(3)
+        last_product(2)
+        finish(0)
+        change(3)
+        finish(1)
+        last_product(3)
+        finish(2)
+        finish(3)

@@ -1,6 +1,7 @@
 from contextlib import ExitStack
 
 import concourse.mybir as mybir
+from concourse.masks import make_identity
 
 K, T, S, H, N = 512, 2048, 512, 512, 512
 FLOPS = 2 * K * H * S * 2 + 2 * H * N * S
@@ -21,6 +22,7 @@ HALF = 256
 BLK = 128
 NBLK = S // BLK
 LIST = 16
+KEPT = (NBLK - 1) * BLK
 
 
 def tile_picked_upwind2_none_p_kernel(
@@ -31,8 +33,8 @@ def tile_picked_upwind2_none_p_kernel(
         keep = ctx.enter_context(tc.tile_pool(name="keep", bufs=1))
         psum = ctx.enter_context(tc.psum_pool(name="psum", bufs=1))
 
-        def tile(name, shape, dtype):
-            return keep.tile(shape, dtype, name=name, align_bytes=64)
+        def tile(name, shape, dtype, tag=None):
+            return keep.tile(shape, dtype, name=name, tag=tag or name, align_bytes=64)
 
         def bank(i, shape):
             return psum.tile(shape, F32, name="bank%d" % i, tag="bank%d" % i)
@@ -45,28 +47,26 @@ def tile_picked_upwind2_none_p_kernel(
         xs = tile("xs", [P, T], U8)
         gain = tile("gain", [P, PACK], F32)
 
+        def load_half(name, w, h):
+            raw = tile("%s_raw%d" % (name, h), [P, PACK, HALF], F32)
+            nc.sync.dma_start(raw[:], w.rearrange("(p j) c -> p j c", j=PACK)[:, :, h * HALF : (h + 1) * HALF])
+            return raw
+
         nc.vector.memset(xs[:].bitcast(I32), 0)
+        nc.gpsimd.dma_start(gain[:], gn.rearrange("(p t) o -> p (t o)", t=PACK))
+        ident = tile("ident", [P, P], F32)
+        make_identity(nc, ident[:])
         nc.sync.dma_start(offs_t[:], offs)
+        w1_raw = [load_half("w1", w1, 0)]
+        nc.sync.dma_start(two_t[:], two)
         for q in range(4):
             nc.sync.dma_start(xs[32 * q : 32 * q + 4, :].bitcast(I32), x_scales[0, 4 * q : 4 * q + 4, :].bitcast(I32))
-        nc.sync.dma_start(two_t[:], two)
-        nc.gpsimd.dma_start(gain[:], gn.rearrange("(p t) o -> p (t o)", t=PACK))
-
-        def load_halves(name, w):
-            halves = []
-            rows = w.rearrange("(p j) c -> p j c", j=PACK)
-            for h in range(2):
-                raw = tile("%s_raw%d" % (name, h), [P, PACK, HALF], F32)
-                nc.sync.dma_start(raw[:], rows[:, :, h * HALF : (h + 1) * HALF])
-                halves.append(raw)
-            return halves
-
-        w1_raw = load_halves("w1", w1)
+        w1_raw.append(load_half("w1", w1, 1))
         nc.sync.dma_start(xw[:].bitcast(I32), x_words[0].rearrange("p n t -> p (n t)").bitcast(I32))
         nc.sync.dma_start(lf_t[:], lf)
         nc.sync.dma_start(rt_t[:], rt)
-        w2_raw = load_halves("w2", w2)
-        w3_raw = load_halves("w3", w3)
+        w2_raw = [load_half("w2", w2, h) for h in range(2)]
+        w3_raw = [load_half("w3", w3, h) for h in range(2)]
         res_t = tile("res_t", [P, PACK, S], F32)
         nc.sync.dma_start(res_t[:], res.rearrange("(g p) j -> p g j", p=P))
 
@@ -103,40 +103,46 @@ def tile_picked_upwind2_none_p_kernel(
 
         gpos = tile("gpos", [P, PACK], F32)
         gneg = tile("gneg", [P, PACK], F32)
-        nc.vector.tensor_scalar(gpos[:], gain[:], 0.75, None, ALU.mult)
-        nc.vector.tensor_scalar(gneg[:], gain[:], -0.75, None, ALU.mult)
+        nc.gpsimd.tensor_scalar(gpos[:], gain[:], 0.75, 0.0, ALU.mult, ALU.add)
+        nc.gpsimd.tensor_scalar(gneg[:], gain[:], -0.75, 0.0, ALU.mult, ALU.add)
 
         w1_bf = [deal("w1", w1_raw, u) for u in range(2)]
         w1q = [quantize("w1q%d" % u, w1_bf[u][:].rearrange("p e m j -> p (e m j)"), HALF) for u in range(2)]
-        nc.vector.tensor_copy(xq[0][:], xw[:].indirect(offs_t[:]))
+        for h in range(2):
+            nc.vector.tensor_copy(xq[0][:, h * HALF : (h + 1) * HALF], xw[:].indirect(offs_t[:, h * HALF // LIST : (h + 1) * HALF // LIST]))
         nc.vector.tensor_copy(x2[0][:], xw[:].indirect(two_t[:]))
 
-        ypos, yneg = [], []
-        for t in range(PACK):
-            y = bank(t, [P, S])
-            product(y[:], w1q[t // 2], slice(P * (t % 2), P * (t % 2 + 1)), xq, slice(0, S))
-            yp = tile("ypos%d" % t, [P, S], F32)
-            yn = tile("yneg%d" % t, [P, S], F32)
-            nc.scalar.activation(yp[:], y[:], COPY, scale=gpos[:, t : t + 1])
-            nc.scalar.activation(yn[:], y[:], COPY, scale=gneg[:, t : t + 1])
-            ypos.append(yp)
-            yneg.append(yn)
+        ypos = [tile("ypos%d" % t, [P, S], F32) for t in range(PACK)]
+        yneg = [tile("yneg%d" % t, [P, S], F32) for t in range(PACK)]
 
-        dl = tile("dl", [P, PACK, S], F32)
-        dr = tile("dr", [P, PACK, S], F32)
+        def project(t, places, bank_no):
+            y = bank(bank_no, [P, places.stop - places.start])
+            product(y[:], w1q[t // 2], slice(P * (t % 2), P * (t % 2 + 1)), xq, places)
+            nc.scalar.activation(ypos[t][:, places], y[:], COPY, scale=gpos[:, t : t + 1])
+            nc.scalar.activation(yneg[t][:, places], y[:], COPY, scale=gneg[:, t : t + 1])
+
+        project(0, slice(0, HALF), 0)
+        project(0, slice(HALF, S), 1)
+        project(1, slice(0, S), 2)
+        project(2, slice(0, S), 3)
+        w2_bf = [deal("w2", w2_raw, 0)]
+        project(3, slice(0, S), 0)
+        w2_bf.append(deal("w2", w2_raw, 1))
+
+        dl = tile("dl", [P, PACK, KEPT], F32)
+        dr = tile("dr", [P, PACK, KEPT], F32)
 
         def left(t, a, b):
-            nc.vector.tensor_tensor(dl[:, t, a:b], ypos[t][:].indirect(lf_t[:, a // LIST : b // LIST]), yneg[t][:, a:b], ALU.add)
+            nc.vector.tensor_tensor(dl[:, t, a % KEPT : a % KEPT + b - a], ypos[t][:].indirect(lf_t[:, a // LIST : b // LIST]), yneg[t][:, a:b], ALU.add)
 
         def right(t, a, b):
-            nc.vector.tensor_tensor(dr[:, t, a:b], yneg[t][:].indirect(rt_t[:, a // LIST : b // LIST]), ypos[t][:, a:b], ALU.add)
+            nc.vector.tensor_tensor(dr[:, t, a % KEPT : a % KEPT + b - a], yneg[t][:].indirect(rt_t[:, a // LIST : b // LIST]), ypos[t][:, a:b], ALU.add)
 
         def differences(t):
-            for h in range(2):
-                left(t, h * HALF, (h + 1) * HALF)
-                right(t, h * HALF, (h + 1) * HALF)
+            for a, b in ((0, HALF), (HALF, HALF + BLK)):
+                left(t, a, b)
+                right(t, a, b)
 
-        w2_bf = [deal("w2", w2_raw, u) for u in range(2)]
         w3_bf = tile("w3_bf", [P, N, PACK], BF16)
         for h in range(2):
             nc.scalar.copy(
@@ -154,7 +160,7 @@ def tile_picked_upwind2_none_p_kernel(
                 product(c[:, t, :], w2q[t // 2], slice(P * (t % 2), P * (t % 2 + 1)), x2, slice(b * BLK, (b + 1) * BLK))
             wind.append(c)
         differences(2)
-        w3q = quantize("w3q", w3_bf[:].rearrange("p n j -> p (n j)"), N)
+        differences(3)
 
         from_left, from_right, z_bf, sums = {}, {}, {}, {}
 
@@ -163,14 +169,14 @@ def tile_picked_upwind2_none_p_kernel(
 
         def term_left(b):
             from_left[b] = tile("from_left%d" % b, [P, PACK, BLK], F32)
-            nc.vector.scalar_tensor_tensor(from_left[b][:], wind[b][:], 0.0, dl[:, :, cols(b)], ALU.max, ALU.mult)
+            nc.vector.scalar_tensor_tensor(from_left[b][:], wind[b][:], 0.0, dl[:, :, cols(b % (NBLK - 1))], ALU.max, ALU.mult)
 
         def term_right(b):
             from_right[b] = tile("from_right%d" % b, [P, PACK, BLK], F32)
-            nc.vector.scalar_tensor_tensor(from_right[b][:], wind[b][:], 0.0, dr[:, :, cols(b)], ALU.min, ALU.mult)
+            nc.vector.scalar_tensor_tensor(from_right[b][:], wind[b][:], 0.0, dr[:, :, cols(b % (NBLK - 1))], ALU.min, ALU.mult)
 
         def change(b):
-            z_bf[b] = tile("z_bf%d" % b, [P, BLK, PACK], BF16)
+            z_bf[b] = tile("z_bf%d" % b, [P, BLK, PACK], BF16, "shared" if b % 2 else None)
             nc.vector.tensor_tensor(
                 z_bf[b][:].rearrange("p (c i) t -> p c t i", i=2),
                 from_left[b][:].rearrange("p t (c i) -> p c t i", i=2),
@@ -178,37 +184,60 @@ def tile_picked_upwind2_none_p_kernel(
                 ALU.add,
             )
 
+        def change_on_tensor(b):
+            turned = bank(b % 2, [P, PACK, P])
+            for t in range(PACK):
+                nc.tensor.matmul(turned[:, t, :], from_left[b][:, t, :], ident[:], start=True, stop=False, is_transpose=True)
+                nc.tensor.matmul(turned[:, t, :], from_right[b][:, t, :], ident[:], start=False, stop=True, is_transpose=True)
+            rounded = tile("rounded%d" % b, [P, 2, P, 2], BF16)
+            nc.scalar.copy(rounded[:], turned[:].rearrange("j (u e) p -> j u p e", e=2))
+            pairs = rounded[:].rearrange("j u p e -> j (u p e)").bitcast(F32)
+            back = bank(2 + b % 2, [P, 2, BLK])
+            for u in range(2):
+                nc.tensor.transpose(back[:, u, :], pairs[:, P * u : P * (u + 1)], ident[:])
+            z_bf[b] = tile("z_bf%d" % b, [P, BLK, PACK], BF16, "shared" if b % 2 else None)
+            nc.scalar.copy(
+                z_bf[b][:].rearrange("p j t -> p (j t)").bitcast(F32).rearrange("p (j u) -> p j u", u=2),
+                back[:].rearrange("p u j -> p j u"),
+            )
+
         def last_product(b):
             zq = quantize("zq%d" % b, z_bf[b][:].rearrange("p j t -> p (j t)"), BLK)
-            sums[b] = bank(b, [P, PACK, BLK])
+            sums[b] = bank(PACK + b, [P, PACK, BLK])
             for g in range(PACK):
                 product(sums[b][:, g, :], w3q, slice(P * g, P * (g + 1)), zq, slice(0, BLK))
 
-        def finish(b):
-            o = tile("o%d" % b, [P, PACK, BLK], F32)
-            nc.vector.tensor_tensor(o[:], sums[b][:], res_t[:, :, cols(b)], ALU.add)
-            nc.sync.dma_start(out.rearrange("(g p) j -> p g j", p=P)[:, :, cols(b)], o[:])
+        def finish(b, o):
+            nc.vector.tensor_tensor(o, sums[b][:], res_t[:, :, cols(b)], ALU.add)
+            nc.sync.dma_start(out.rearrange("(g p) j -> p g j", p=P)[:, :, cols(b)], o)
 
-        last = PACK - 1
-        for b in range(2):
-            left(last, b * BLK, (b + 1) * BLK)
-            right(last, b * BLK, (b + 1) * BLK)
-        for b in range(2):
-            term_left(b)
-            term_right(b)
-            left(last, (b + 2) * BLK, (b + 3) * BLK)
-            change(b)
-            right(last, (b + 2) * BLK, (b + 3) * BLK)
-            last_product(b)
+        def late(t):
+            left(t, KEPT, S)
+            right(t, KEPT, S)
+
+        term_left(0)
+        term_right(0)
+        change_on_tensor(0)
+        w3q = quantize("w3q", w3_bf[:].rearrange("p n j -> p (n j)"), N)
+        term_left(1)
+        term_right(1)
+        change_on_tensor(1)
         term_left(2)
         term_right(2)
-        term_left(3)
+        late(0)
         change(2)
-        term_right(3)
+        late(1)
         last_product(2)
-        finish(0)
+        late(2)
+        last_product(0)
+        late(3)
+        term_left(3)
+        term_right(3)
+        last_product(1)
         change(3)
-        finish(1)
+        finish(2, tile("o2", [P, PACK, BLK], F32)[:])
         last_product(3)
-        finish(2)
-        finish(3)
+        o01 = tile("o01", [P, 2, PACK, BLK], F32, "shared")
+        finish(0, o01[:, 0])
+        finish(1, o01[:, 1])
+        finish(3, tile("o3", [P, PACK, BLK], F32)[:])

from contextlib import ExitStack

import concourse.mybir as mybir
from concourse.masks import make_identity

K, T, S, H, N = 512, 2048, 512, 512, 512
FLOPS = 2 * K * H * S * 2 + 2 * H * N * S

F32 = mybir.dt.float32
BF16 = mybir.dt.bfloat16
I32 = mybir.dt.int32
U32 = mybir.dt.uint32
U16 = mybir.dt.uint16
U8 = mybir.dt.uint8
FP8X4 = mybir.dt.float8_e4m3fn_x4
ALU = mybir.AluOpType
COPY = mybir.ActivationFunctionType.Copy

P = 128
PACK = 4
HALF = 256
BLK = 128
NBLK = S // BLK
LIST = 16
KEPT = (NBLK - 1) * BLK


def tile_picked_upwind2_none_p_kernel(
    tc, x_words, x_scales, w1, w2, gn, w3, res, offs, two, lf, rt, out
):
    nc = tc.nc
    with ExitStack() as ctx:
        keep = ctx.enter_context(tc.tile_pool(name="keep", bufs=1))
        psum = ctx.enter_context(tc.psum_pool(name="psum", bufs=1))

        def tile(name, shape, dtype, tag=None):
            return keep.tile(shape, dtype, name=name, tag=tag or name, align_bytes=64)

        def bank(i, shape):
            return psum.tile(shape, F32, name="bank%d" % i, tag="bank%d" % i)

        offs_t = tile("offs_t", [P, S // LIST], U16)
        two_t = tile("two_t", [P, S // LIST], U16)
        lf_t = tile("lf_t", [P, S // LIST], U16)
        rt_t = tile("rt_t", [P, S // LIST], U16)
        xw = tile("xw", [P, T], U32)
        xs = tile("xs", [P, T], U8)
        gain = tile("gain", [P, PACK], F32)

        def load_half(name, w, h):
            raw = tile("%s_raw%d" % (name, h), [P, PACK, HALF], F32)
            nc.sync.dma_start(raw[:], w.rearrange("(p j) c -> p j c", j=PACK)[:, :, h * HALF : (h + 1) * HALF])
            return raw

        nc.vector.memset(xs[:].bitcast(I32), 0)
        nc.gpsimd.dma_start(gain[:], gn.rearrange("(p t) o -> p (t o)", t=PACK))
        ident = tile("ident", [P, P], F32)
        make_identity(nc, ident[:])
        nc.sync.dma_start(offs_t[:], offs)
        w1_raw = [load_half("w1", w1, 0)]
        nc.sync.dma_start(two_t[:], two)
        for q in range(4):
            nc.sync.dma_start(xs[32 * q : 32 * q + 4, :].bitcast(I32), x_scales[0, 4 * q : 4 * q + 4, :].bitcast(I32))
        w1_raw.append(load_half("w1", w1, 1))
        nc.sync.dma_start(xw[:].bitcast(I32), x_words[0].rearrange("p n t -> p (n t)").bitcast(I32))
        nc.sync.dma_start(lf_t[:], lf)
        nc.sync.dma_start(rt_t[:], rt)
        w2_raw = [load_half("w2", w2, h) for h in range(2)]
        w3_raw = [load_half("w3", w3, h) for h in range(2)]
        res_t = tile("res_t", [P, PACK, S], F32)
        nc.sync.dma_start(res_t[:], res.rearrange("(g p) j -> p g j", p=P))

        def deal(name, raw, u):
            dealt = tile("%s_bf%d" % (name, u), [P, 2, P, PACK], BF16)
            for h in range(2):
                nc.scalar.copy(
                    dealt[:].rearrange("p e m j -> p m j e")[:, 64 * h : 64 * h + 64],
                    raw[h][:].rearrange("p j (m u e) -> p u m j e", u=2, e=2)[:, u],
                )
            return dealt

        def quantize(name, src, width):
            codes = tile(name + "_codes", [P, width], U32)
            scales = tile(name + "_scales", [P, width], U8)
            nc.vector.quantize_mx(out=codes[:].bitcast(FP8X4), scales=scales[:], in_=src)
            return codes, scales

        def product(dst, lhs, lhs_cols, rhs, rhs_cols):
            nc.tensor.matmul_mx(
                out=dst,
                lhsT=lhs[0][:, lhs_cols].bitcast(FP8X4),
                lhsT_scale=lhs[1][:, lhs_cols],
                rhs=rhs[0][:, rhs_cols].bitcast(FP8X4),
                rhs_scale=rhs[1][:, rhs_cols],
                start=True,
                stop=True,
            )

        xq = (tile("xq_w", [P, S], U32), tile("xq_s", [P, S], U8))
        x2 = (tile("x2_w", [P, S], U32), tile("x2_s", [P, S], U8))
        nc.vector.tensor_copy(xq[1][:], xs[:].indirect(offs_t[:]))
        nc.vector.tensor_copy(x2[1][:], xs[:].indirect(two_t[:]))

        gpos = tile("gpos", [P, PACK], F32)
        gneg = tile("gneg", [P, PACK], F32)
        nc.gpsimd.tensor_scalar(gpos[:], gain[:], 0.75, 0.0, ALU.mult, ALU.add)
        nc.gpsimd.tensor_scalar(gneg[:], gain[:], -0.75, 0.0, ALU.mult, ALU.add)

        w1_bf = [deal("w1", w1_raw, u) for u in range(2)]
        w1q = [quantize("w1q%d" % u, w1_bf[u][:].rearrange("p e m j -> p (e m j)"), HALF) for u in range(2)]
        for h in range(2):
            nc.vector.tensor_copy(xq[0][:, h * HALF : (h + 1) * HALF], xw[:].indirect(offs_t[:, h * HALF // LIST : (h + 1) * HALF // LIST]))
        nc.vector.tensor_copy(x2[0][:], xw[:].indirect(two_t[:]))

        ypos = [tile("ypos%d" % t, [P, S], F32) for t in range(PACK)]
        yneg = [tile("yneg%d" % t, [P, S], F32) for t in range(PACK)]

        def project(t, places, bank_no):
            y = bank(bank_no, [P, places.stop - places.start])
            product(y[:], w1q[t // 2], slice(P * (t % 2), P * (t % 2 + 1)), xq, places)
            nc.scalar.activation(ypos[t][:, places], y[:], COPY, scale=gpos[:, t : t + 1])
            nc.scalar.activation(yneg[t][:, places], y[:], COPY, scale=gneg[:, t : t + 1])

        project(0, slice(0, HALF), 0)
        project(0, slice(HALF, S), 1)
        project(1, slice(0, S), 2)
        project(2, slice(0, S), 3)
        w2_bf = [deal("w2", w2_raw, 0)]
        project(3, slice(0, S), 0)
        w2_bf.append(deal("w2", w2_raw, 1))

        dl = tile("dl", [P, PACK, KEPT], F32)
        dr = tile("dr", [P, PACK, KEPT], F32)

        def left(t, a, b):
            nc.vector.tensor_tensor(dl[:, t, a % KEPT : a % KEPT + b - a], ypos[t][:].indirect(lf_t[:, a // LIST : b // LIST]), yneg[t][:, a:b], ALU.add)

        def right(t, a, b):
            nc.vector.tensor_tensor(dr[:, t, a % KEPT : a % KEPT + b - a], yneg[t][:].indirect(rt_t[:, a // LIST : b // LIST]), ypos[t][:, a:b], ALU.add)

        def differences(t):
            for a, b in ((0, HALF), (HALF, HALF + BLK)):
                left(t, a, b)
                right(t, a, b)

        w3_bf = tile("w3_bf", [P, N, PACK], BF16)
        for h in range(2):
            nc.scalar.copy(
                w3_bf[:, h * HALF : (h + 1) * HALF, :].rearrange("p (c i) j -> p c j i", i=4),
                w3_raw[h][:].rearrange("p j (c i) -> p c j i", i=4),
            )

        differences(0)
        differences(1)
        w2q = [quantize("w2q%d" % u, w2_bf[u][:].rearrange("p e m j -> p (e m j)"), HALF) for u in range(2)]
        wind = []
        for b in range(NBLK):
            c = bank(PACK + b, [P, PACK, BLK])
            for t in range(PACK):
                product(c[:, t, :], w2q[t // 2], slice(P * (t % 2), P * (t % 2 + 1)), x2, slice(b * BLK, (b + 1) * BLK))
            wind.append(c)
        differences(2)
        differences(3)

        from_left, from_right, z_bf, sums = {}, {}, {}, {}

        def cols(b):
            return slice(b * BLK, (b + 1) * BLK)

        def term_left(b):
            from_left[b] = tile("from_left%d" % b, [P, PACK, BLK], F32)
            nc.vector.scalar_tensor_tensor(from_left[b][:], wind[b][:], 0.0, dl[:, :, cols(b % (NBLK - 1))], ALU.max, ALU.mult)

        def term_right(b):
            from_right[b] = tile("from_right%d" % b, [P, PACK, BLK], F32)
            nc.vector.scalar_tensor_tensor(from_right[b][:], wind[b][:], 0.0, dr[:, :, cols(b % (NBLK - 1))], ALU.min, ALU.mult)

        def change(b):
            z_bf[b] = tile("z_bf%d" % b, [P, BLK, PACK], BF16, "shared" if b % 2 else None)
            nc.vector.tensor_tensor(
                z_bf[b][:].rearrange("p (c i) t -> p c t i", i=2),
                from_left[b][:].rearrange("p t (c i) -> p c t i", i=2),
                from_right[b][:].rearrange("p t (c i) -> p c t i", i=2),
                ALU.add,
            )

        def change_on_tensor(b):
            turned = bank(b % 2, [P, PACK, P])
            for t in range(PACK):
                nc.tensor.matmul(turned[:, t, :], from_left[b][:, t, :], ident[:], start=True, stop=False, is_transpose=True)
                nc.tensor.matmul(turned[:, t, :], from_right[b][:, t, :], ident[:], start=False, stop=True, is_transpose=True)
            rounded = tile("rounded%d" % b, [P, 2, P, 2], BF16)
            nc.scalar.copy(rounded[:], turned[:].rearrange("j (u e) p -> j u p e", e=2))
            pairs = rounded[:].rearrange("j u p e -> j (u p e)").bitcast(F32)
            back = bank(2 + b % 2, [P, 2, BLK])
            for u in range(2):
                nc.tensor.transpose(back[:, u, :], pairs[:, P * u : P * (u + 1)], ident[:])
            z_bf[b] = tile("z_bf%d" % b, [P, BLK, PACK], BF16, "shared" if b % 2 else None)
            nc.scalar.copy(
                z_bf[b][:].rearrange("p j t -> p (j t)").bitcast(F32).rearrange("p (j u) -> p j u", u=2),
                back[:].rearrange("p u j -> p j u"),
            )

        def last_product(b):
            zq = quantize("zq%d" % b, z_bf[b][:].rearrange("p j t -> p (j t)"), BLK)
            sums[b] = bank(PACK + b, [P, PACK, BLK])
            for g in range(PACK):
                product(sums[b][:, g, :], w3q, slice(P * g, P * (g + 1)), zq, slice(0, BLK))

        def finish(b, o):
            nc.vector.tensor_tensor(o, sums[b][:], res_t[:, :, cols(b)], ALU.add)
            nc.sync.dma_start(out.rearrange("(g p) j -> p g j", p=P)[:, :, cols(b)], o)

        def late(t):
            left(t, KEPT, S)
            right(t, KEPT, S)

        term_left(0)
        term_right(0)
        change_on_tensor(0)
        w3q = quantize("w3q", w3_bf[:].rearrange("p n j -> p (n j)"), N)
        term_left(1)
        term_right(1)
        change_on_tensor(1)
        term_left(2)
        term_right(2)
        late(0)
        change(2)
        late(1)
        last_product(2)
        late(2)
        last_product(0)
        late(3)
        term_left(3)
        term_right(3)
        last_product(1)
        change(3)
        finish(2, tile("o2", [P, PACK, BLK], F32)[:])
        last_product(3)
        o01 = tile("o01", [P, 2, PACK, BLK], F32, "shared")
        finish(0, o01[:, 0])
        finish(1, o01[:, 1])
        finish(3, tile("o3", [P, PACK, BLK], F32)[:])
